import numpy as np
import ml_dtypes


def mxq(x, axis, fmt="e4m3"):
    dtype, down = {"e4m3": (ml_dtypes.float8_e4m3fn, 7), "e5m2": (ml_dtypes.float8_e5m2, 14)}[fmt]
    v = np.moveaxis(np.asarray(x, np.float32).astype(ml_dtypes.bfloat16).astype(np.float64), axis, -1)
    blocks = v.reshape(v.shape[:-1] + (-1, 32))
    amax = np.abs(blocks).max(-1, keepdims=True)
    byte = np.maximum(np.where(amax > 0, np.frexp(amax)[1] - 1 + 127, 0) - down, 1)
    scale = np.exp2(byte - 127.0)
    codes = (blocks / scale).astype(np.float32).astype(dtype).astype(np.float64)
    return np.moveaxis((codes * scale).reshape(v.shape), -1, axis)


WIDE = False


def mx_kscale(k):
    if not WIDE:
        return np.ones(k)
    levels = np.array([10, -10, 5, -5, 0])
    if k % 512:
        return np.exp2(np.random.permutation(np.resize(levels, k // 32))).repeat(32)
    a = np.empty((k // 512, 16))
    for p in range(k // 512):
        a[p, :8] = np.random.permutation(np.resize(levels, 8))
        for g in range(8):
            far = levels[np.abs(levels - a[p, g]) >= 10]
            a[p, g + 8] = far[np.random.randint(len(far))]
    return np.exp2(a.ravel()).repeat(32)


def f64(x):
    return np.asarray(x).astype(np.float64)


def striped(idx):
    return np.tile(idx.reshape(-1, 16).T, (8, 1)).astype(np.uint16)


def unstriped(offs):
    return offs[:16].T.reshape(-1).astype(np.int64)


def striped8(idx):
    return np.concatenate([x.reshape(-1, 16).T for x in idx]).astype(np.uint16)


def runs(offs, k):
    lists = np.stack([offs[16 * r : 16 * r + 16].T.reshape(-1) for r in range(8)]).astype(np.int64)
    return lists[np.arange(k) % 512 // 64]


def pack_weight(w):
    k, n = w.shape
    w = f64(np.asarray(w, np.float32).astype(ml_dtypes.bfloat16)).reshape(k // 32, 32, n)
    amax = np.abs(w).max(1)
    byte = np.clip(np.where(amax > 0, np.frexp(amax)[1] - 1 + 127 - 7, 1), 1, 254)
    scaled = (w * np.exp2(127.0 - byte)[:, None, :]).reshape(k, n).astype(np.float32)
    words = np.ascontiguousarray(scaled.reshape(k // 512, 128, 4, n).transpose(0, 1, 3, 2)).astype(ml_dtypes.float8_e4m3fn).view(np.uint8)
    return words, np.ascontiguousarray(byte.astype(np.uint8).reshape(k // 512, 16, n))


def unpack_weight(words, scales):
    g, p, n, _ = words.shape
    vals = np.ascontiguousarray(words).view(ml_dtypes.float8_e4m3fn).astype(np.float64) * np.repeat(np.exp2(scales.astype(np.float64) - 127.0), 8, axis=1)[..., None]
    return vals.transpose(0, 1, 3, 2).reshape(g * 512, n)


E2M1 = np.array([0.0, 0.5, 1.0, 1.5, 2.0, 3.0, 4.0, 6.0, -0.0, -0.5, -1.0, -1.5, -2.0, -3.0, -4.0, -6.0])


def pack_fp4(w):
    k, n = w.shape
    w = f64(np.asarray(w, np.float32).astype(ml_dtypes.bfloat16)).reshape(k // 32, 32, n)
    amax = np.abs(w).max(1)
    mant, ex = np.frexp(amax / 6.0)
    byte = np.clip(np.where(amax > 0, np.where(mant > 0.5, ex, ex - 1) + 127, 1), 1, 254)
    scaled = (w * np.exp2(127.0 - byte)[:, None, :]).reshape(k, n).astype(np.float32)
    c = np.ascontiguousarray(scaled.reshape(k // 512, 128, 4, n).transpose(0, 1, 3, 2)).astype(ml_dtypes.float4_e2m1fn).view(np.uint8) & 0xF
    words = (c[..., 0::2] | (c[..., 1::2] << 4)).reshape(k // 512, 128, 2 * n)
    return np.ascontiguousarray(words), np.ascontiguousarray(byte.astype(np.uint8).reshape(k // 512, 16, n))


def unpack_fp4(words, scales):
    g, _, n = scales.shape
    words = np.ascontiguousarray(words).reshape(g, 128, n, 2)
    nib = np.empty((g, 128, n, 4), np.uint8)
    nib[..., 0::2] = words & 0xF
    nib[..., 1::2] = words >> 4
    vals = E2M1[nib] * np.repeat(np.exp2(scales.astype(np.float64) - 127.0), 8, axis=1)[..., None]
    return vals.transpose(0, 1, 3, 2).reshape(g * 512, n)


def sigmoid(v):
    return 1.0 / (1.0 + np.exp(-np.maximum(v, -700.0)))

def planes(y):
    n, m = y.shape
    v = y.astype(np.float32).astype(ml_dtypes.bfloat16).astype(np.float64).reshape(n // 32, 32, m)
    top = np.abs(v).max(1)
    byte = np.clip(np.where(top > 0, np.frexp(top)[1] - 1 + 127 - 7, 1), 1, 254)
    codes = (v * np.exp2(127.0 - byte)[:, None, :]).reshape(n, m).astype(np.float32).astype(ml_dtypes.float8_e4m3fn).view(np.uint8)
    words = codes.reshape(n // 512, 128, 4, m).transpose(0, 1, 3, 2)
    return np.ascontiguousarray(words), np.ascontiguousarray(byte.astype(np.uint8).reshape(n // 512, 16, m))


K, T, S, N, H = 512, 2048, 512, 512, 512


def setup_inputs():
    n = np.random.standard_normal
    s = mx_kscale(K)[:, None]
    u = mx_kscale(H)
    packed_xT = pack_weight(n((K, T)) * s)
    packed_w1 = pack_fp4(n((K, H)) / np.sqrt(K) / s)
    packed_w2 = pack_fp4(n((K, H)) / np.sqrt(K) / s)
    packed_w3 = pack_fp4(n((H, N)) / np.sqrt(H) / u[:, None])
    return {
        "x_words": packed_xT[0],
        "x_scales": packed_xT[1],
        "w1_words": packed_w1[0],
        "w1_scales": packed_w1[1],
        "w2_words": packed_w2[0],
        "w2_scales": packed_w2[1],
        "gn": (np.random.uniform(0.5, 1.5, (H, 1)) * u[:, None]).astype(np.float32),
        "w3_words": packed_w3[0],
        "w3_scales": packed_w3[1],
        "offs": striped(np.random.permutation(T)[:S]),
        "two": striped(np.random.permutation(T)[:S]),
        "n1": striped8(np.stack([np.random.permutation(S) for _ in range(8)])),
        "n2": striped8(np.stack([np.random.permutation(S) for _ in range(8)])),
        "n3": striped8(np.stack([np.random.permutation(S) for _ in range(8)])),
        "n4": striped8(np.stack([np.random.permutation(S) for _ in range(8)])),
        "n5": striped8(np.stack([np.random.permutation(S) for _ in range(8)])),
    }


def reference(x_words, x_scales, w1_words, w1_scales, w2_words, w2_scales, gn, w3_words, w3_scales, offs, two, n1, n2, n3, n4, n5):
    xq = unpack_weight(x_words, x_scales)[:, unstriped(offs)]
    y = unpack_fp4(w1_words, w1_scales).T @ xq
    x_two = unpack_weight(x_words, x_scales)[:, unstriped(two)]
    d = unpack_fp4(w2_words, w2_scales).T @ x_two
    z = f64(gn) * (y + (sigmoid(d[np.arange(H)[:, None], runs(n2, H)] - d)) * (y[np.arange(H)[:, None], runs(n1, H)] - y))
    h = unpack_fp4(w3_words, w3_scales).T @ mxq(z, 0, "e4m3")
    pa = h[np.arange(N)[:, None], runs(n3, N)]
    out_0 = pa + (sigmoid(h[np.arange(N)[:, None], runs(n4, N)])) * (h[np.arange(N)[:, None], runs(n5, N)] - pa)
    return (out_0,) + planes(out_0)

@@ -1,0 +1,225 @@
+from contextlib import ExitStack
+
+import concourse.mybir as mybir
+
+K, T, S, H, N = 512, 2048, 512, 512, 512
+FLOPS = 2 * K * H * S * 2 + 2 * H * N * S
+
+F32 = mybir.dt.float32
+BF16 = mybir.dt.bfloat16
+I32 = mybir.dt.int32
+U32 = mybir.dt.uint32
+U16 = mybir.dt.uint16
+U8 = mybir.dt.uint8
+FP8X4 = mybir.dt.float8_e4m3fn_x4
+FP4X4 = mybir.dt.float4_e2m1fn_x4
+ALU = mybir.AluOpType
+ACT = mybir.ActivationFunctionType
+
+P = 128
+PACK = 4
+HALVES = [(0, 256), (256, 512)]
+Z_PIECES = [(0, 256), (256, 384), (384, 512)]
+OUT_PIECES = [(0, 256), (256, 384), (384, 512)]
+
+
+def entries(list_tile, lo, hi):
+    return list_tile[:, lo // 16 : hi // 16]
+
+
+def load_scale_rows(queue, plane, scales):
+    for q in range(4):
+        queue.dma_start(out=plane[32 * q : 32 * q + 4, :].bitcast(I32), in_=scales[0, 4 * q : 4 * q + 4, :].bitcast(I32))
+
+
+def deal_words(eng, words, raw_words):
+    eng.tensor_copy(
+        out=words[:].rearrange("p (t m b) -> p t m b", t=PACK, b=2),
+        in_=raw_words[:].rearrange("p (m t b) -> p t m b", t=PACK, b=2),
+    )
+
+
+def deal_plane(eng, plane, raw_plane):
+    eng.tensor_copy(
+        out=plane[:].rearrange("p (t m) -> p t m", t=PACK),
+        in_=raw_plane[:].rearrange("p (m t) -> p t m", t=PACK),
+    )
+
+
+def product(nc, acc, words, plane, t, codes, scales):
+    nc.tensor.matmul_mx(
+        out=acc,
+        lhsT=words[:, 2 * P * t : 2 * P * (t + 1)].bitcast(FP4X4),
+        lhsT_scale=plane[:, P * t : P * (t + 1)],
+        rhs=codes.bitcast(FP8X4),
+        rhs_scale=scales,
+        start=True,
+        stop=True,
+    )
+
+
+def woven(tile):
+    return tile[:].rearrange("p (c i t) -> p c t i", t=PACK, i=2)
+
+
+def by_pairs(ap):
+    return ap.rearrange("p t (c i) -> p c t i", i=2)
+
+
+def tile_picked_twlpullblerp_none_po_kernel(
+    tc, x_words, x_scales, w1_words, w1_scales, w2_words, w2_scales, gn, w3_words, w3_scales,
+    offs, two, n1, n2, n3, n4, n5, out_0, out_1, out_2,
+):
+    nc = tc.nc
+    with ExitStack() as ctx:
+        keep = ctx.enter_context(tc.tile_pool(name="keep", bufs=1))
+        psum = ctx.enter_context(tc.psum_pool(name="psum", bufs=1))
+
+        def load_list(src, name):
+            lst = keep.tile([P, S // 16], U16, name=name)
+            nc.sync.dma_start(lst[:], src)
+            return lst
+
+        def load_words(src, name):
+            raw = keep.tile([P, 2 * H], U8, name=name, align_bytes=64)
+            nc.sync.dma_start(out=raw[:].bitcast(I32), in_=src[0].bitcast(I32))
+            return raw
+
+        x_plane = keep.tile([P, T], U8, align_bytes=64)
+        nc.vector.memset(x_plane[:].bitcast(I32), 0)
+        raw_planes = [keep.tile([P, H], U8, name="raw_plane%d" % i, align_bytes=64) for i in range(2)]
+        for rp in raw_planes[::-1]:
+            nc.vector.memset(rp[:].bitcast(I32), 0)
+
+        load_scale_rows(nc.sync, x_plane, x_scales)
+        two_l = load_list(two, "two_l")
+        w2_raw = load_words(w2_words, "w2_raw")
+        offs_l = load_list(offs, "offs_l")
+        x_table = keep.tile([P, T], I32, align_bytes=64)
+        nc.sync.dma_start(out=x_table[:], in_=x_words[0].rearrange("p n t -> p (n t)").bitcast(I32))
+        load_scale_rows(nc.sync, raw_planes[1], w2_scales)
+        w1_raw = load_words(w1_words, "w1_raw")
+        load_scale_rows(nc.sync, raw_planes[0], w1_scales)
+        n2_l = load_list(n2, "n2_l")
+        gain = keep.tile([P, PACK], F32)
+        nc.sync.dma_start(out=gain[:], in_=gn.rearrange("(p t) o -> p (t o)", t=PACK))
+        n1_l = load_list(n1, "n1_l")
+        n4_l = load_list(n4, "n4_l")
+        n3_l = load_list(n3, "n3_l")
+        n5_l = load_list(n5, "n5_l")
+
+        w_words = [keep.tile([P, 2 * H], U8, name="w_words%d" % i, align_bytes=64) for i in range(3)]
+        w_planes = [keep.tile([P, H], U8, name="w_plane%d" % i, align_bytes=64) for i in range(3)]
+
+        two_codes = keep.tile([P, S], U32, align_bytes=64)
+        two_scales = keep.tile([P, S], U8, align_bytes=64)
+        idx_codes = keep.tile([P, S], U32, align_bytes=64)
+        idx_scales = keep.tile([P, S], U8, align_bytes=64)
+
+        deal_words(nc.vector, w_words[1], w2_raw)
+        nc.vector.tensor_copy(two_codes[:], x_table[:].bitcast(U32).indirect(two_l[:]))
+        nc.vector.tensor_copy(two_scales[:], x_plane[:].indirect(two_l[:]))
+        deal_plane(nc.vector, w_planes[1], raw_planes[1])
+        nc.vector.tensor_copy(idx_codes[:], x_table[:].bitcast(U32).indirect(offs_l[:]))
+        nc.vector.tensor_copy(idx_scales[:], x_plane[:].indirect(offs_l[:]))
+        deal_words(nc.vector, w_words[0], w1_raw)
+        deal_plane(nc.vector, w_planes[0], raw_planes[0])
+        nc.sync.dma_start(out=w2_raw[:].bitcast(I32), in_=w3_words[0].bitcast(I32))
+        load_scale_rows(nc.sync, raw_planes[1], w3_scales)
+
+        d_acc = [psum.tile([P, S], F32, name="d_acc%d" % t, tag="bank%d" % t) for t in range(PACK)]
+        y_acc = [psum.tile([P, S], F32, name="y_acc%d" % t, tag="bank%d" % (PACK + t)) for t in range(PACK)]
+        for t in range(PACK):
+            product(nc, d_acc[t][:], w_words[1], w_planes[1], t, two_codes[:], two_scales[:])
+        for t in range(PACK):
+            product(nc, y_acc[t][:], w_words[0], w_planes[0], t, idx_codes[:], idx_scales[:])
+
+        d_rows = [keep.tile([P, S], F32, name="d_rows%d" % t) for t in range(PACK)]
+        d_here = [keep.tile([P, S], F32, name="d_here%d" % t) for t in range(PACK)]
+        gy_rows = [keep.tile([P, S], F32, name="gy_rows%d" % t) for t in range(PACK)]
+        diff = [keep.tile([P, S], F32, name="diff%d" % t) for t in range(PACK)]
+        pull = [keep.tile([P, S], F32, name="pull%d" % t) for t in range(PACK)]
+        far = keep.tile([P, PACK, S], F32)
+        near = keep.tile([P, PACK, S], F32)
+
+        def gate_input(t):
+            nc.scalar.copy(d_rows[t][:], d_acc[t][:])
+            nc.scalar.copy(d_here[t][:], d_acc[t][:])
+            for lo, hi in HALVES:
+                nc.vector.tensor_tensor(diff[t][:, lo:hi], d_rows[t][:].indirect(entries(n2_l, lo, hi)), d_here[t][:, lo:hi], ALU.subtract)
+
+        def blend_terms(t):
+            nc.scalar.activation(gy_rows[t][:], y_acc[t][:], ACT.Copy, scale=gain[:, t : t + 1])
+            nc.scalar.activation(pull[t][:], diff[t][:], ACT.Sigmoid)
+            for lo, hi in HALVES:
+                nc.vector.tensor_tensor(far[:, t, lo:hi], gy_rows[t][:].indirect(entries(n1_l, lo, hi)), pull[t][:, lo:hi], ALU.mult)
+            nc.vector.scalar_tensor_tensor(near[:, t, :], pull[t][:], 1.0, gy_rows[t][:], ALU.subtract, ALU.mult)
+
+        gate_input(0)
+        for t in range(PACK):
+            if t + 1 < PACK:
+                gate_input(t + 1)
+            blend_terms(t)
+        deal_words(nc.vector, w_words[2], w2_raw)
+        deal_plane(nc.vector, w_planes[2], raw_planes[1])
+
+        h_acc = [psum.tile([P, S], F32, name="h_acc%d" % t, tag="bank%d" % t) for t in range(PACK)]
+        h_rows = [keep.tile([P, S], F32, name="h_rows%d" % t) for t in range(PACK)]
+        z_woven = [keep.tile([P, PACK * (hi - lo)], BF16, name="z_woven%d" % lo, align_bytes=64) for lo, hi in Z_PIECES]
+        z_codes = [keep.tile([P, hi - lo], U32, name="z_codes%d" % lo, align_bytes=64) for lo, hi in Z_PIECES]
+        z_scales = [keep.tile([P, hi - lo], U8, name="z_scales%d" % lo, align_bytes=64) for lo, hi in Z_PIECES]
+
+        def blend(i):
+            lo, hi = Z_PIECES[i]
+            nc.vector.tensor_tensor(woven(z_woven[i]), by_pairs(far[:, :, lo:hi]), by_pairs(near[:, :, lo:hi]), ALU.subtract)
+
+        def last_product(i):
+            lo, hi = Z_PIECES[i]
+            nc.vector.quantize_mx(out=z_codes[i][:].bitcast(FP8X4), scales=z_scales[i][:], in_=z_woven[i][:])
+            for t in range(PACK):
+                product(nc, h_acc[t][:, lo:hi], w_words[2], w_planes[2], t, z_codes[i][:], z_scales[i][:])
+                if hi == S and t == 0:
+                    nc.vector.tensor_copy(h_rows[t][:, lo:hi], h_acc[t][:, lo:hi])
+                else:
+                    nc.scalar.copy(h_rows[t][:, lo:hi], h_acc[t][:, lo:hi])
+
+        blend(0)
+        for i in range(len(Z_PIECES)):
+            if i + 1 < len(Z_PIECES):
+                blend(i + 1)
+            last_product(i)
+
+        out_rows = out_0.rearrange("(p t) j -> p t j", t=PACK)
+        out_words = out_1[0].rearrange("p j r -> p (j r)").bitcast(I32)
+        o_scales = keep.tile([P, S], U8, align_bytes=64)
+        for lo, hi in OUT_PIECES:
+            w = hi - lo
+            result = keep.tile([P, PACK, w], F32, name="result%d" % lo)
+            for t in range(PACK):
+                mix = keep.tile([P, w], F32, name="mix%d_%d" % (lo, t))
+                rest = keep.tile([P, w], F32, name="rest%d_%d" % (lo, t))
+                term5 = keep.tile([P, w], F32, name="term5_%d_%d" % (lo, t))
+                term3 = keep.tile([P, w], F32, name="term3_%d_%d" % (lo, t))
+                nc.scalar.activation(mix[:], h_rows[t][:].indirect(entries(n4_l, lo, hi)), ACT.Sigmoid)
+                if lo == 0 and t == 0:
+                    nc.vector.tensor_copy(term3[:], h_rows[t][:].indirect(entries(n3_l, lo, hi)))
+                    nc.vector.tensor_tensor(rest[:], h_rows[t][:].indirect(entries(n5_l, lo, hi)), term3[:], ALU.subtract)
+                    nc.vector.tensor_tensor(term5[:], rest[:], mix[:], ALU.mult)
+                    nc.vector.tensor_tensor(result[:, t, :], term3[:], term5[:], ALU.add)
+                    continue
+                nc.scalar.activation(rest[:], mix[:], ACT.Copy, scale=-1.0, bias=1.0)
+                nc.vector.tensor_tensor(term5[:], h_rows[t][:].indirect(entries(n5_l, lo, hi)), mix[:], ALU.mult)
+                nc.vector.tensor_tensor(term3[:], h_rows[t][:].indirect(entries(n3_l, lo, hi)), rest[:], ALU.mult)
+                nc.vector.tensor_tensor(result[:, t, :], term3[:], term5[:], ALU.add)
+            nc.sync.dma_start(out=out_rows[:, :, lo:hi], in_=result[:])
+            o_woven = keep.tile([P, PACK * w], BF16, name="o_woven%d" % lo, align_bytes=64)
+            if hi < S:
+                nc.scalar.copy(woven(o_woven), by_pairs(result[:]))
+            else:
+                nc.vector.tensor_copy(woven(o_woven), by_pairs(result[:]))
+            o_codes = keep.tile([P, w], U32, name="o_codes%d" % lo, align_bytes=64)
+            nc.vector.quantize_mx(out=o_codes[:].bitcast(FP8X4), scales=o_scales[:, lo:hi], in_=o_woven[:])
+            nc.sync.dma_start(out=out_words[:, lo:hi], in_=o_codes[:].bitcast(I32))
+        for q in range(4):
+            queue = nc.scalar if q % 2 else nc.sync
+            queue.dma_start(out=out_2[0, 4 * q : 4 * q + 4, :].bitcast(I32), in_=o_scales[32 * q : 32 * q + 4, :].bitcast(I32))

@@ -87,19 +87,24 @@ def tile_picked_twlpullblerp_none_po_kernel(
 
         x_plane = keep.tile([P, T], U8, align_bytes=64)
         nc.vector.memset(x_plane[:].bitcast(I32), 0)
-        raw_planes = [keep.tile([P, H], U8, name="raw_plane%d" % i, align_bytes=64) for i in range(2)]
-        for rp in raw_planes[::-1]:
-            nc.vector.memset(rp[:].bitcast(I32), 0)
+        w2_raw_plane = keep.tile([P, H], U8, tag="after_w2_plane", align_bytes=64)
+        nc.vector.memset(w2_raw_plane[:].bitcast(I32), 0)
+        raw_plane = keep.tile([P, H], U8, align_bytes=64)
+        nc.vector.memset(raw_plane[:].bitcast(I32), 0)
+        warm = keep.tile([P, 2], F32)
+        nc.gpsimd.memset(warm[:, 0:1], 0.0)
+        nc.scalar.activation(warm[:, 1:2], warm[:, 0:1], ACT.Sigmoid)
 
         load_scale_rows(nc.sync, x_plane, x_scales)
+        x_table = keep.tile([P, T], I32, align_bytes=64)
         two_l = load_list(two, "two_l")
         w2_raw = load_words(w2_words, "w2_raw")
         offs_l = load_list(offs, "offs_l")
-        x_table = keep.tile([P, T], I32, align_bytes=64)
         nc.sync.dma_start(out=x_table[:], in_=x_words[0].rearrange("p n t -> p (n t)").bitcast(I32))
-        load_scale_rows(nc.sync, raw_planes[1], w2_scales)
+        load_scale_rows(nc.sync, w2_raw_plane, w2_scales)
         w1_raw = load_words(w1_words, "w1_raw")
-        load_scale_rows(nc.sync, raw_planes[0], w1_scales)
+        load_scale_rows(nc.sync, raw_plane, w1_scales)
+        w3_raw = load_words(w3_words, "w3_raw")
         n2_l = load_list(n2, "n2_l")
         gain = keep.tile([P, PACK], F32)
         nc.sync.dma_start(out=gain[:], in_=gn.rearrange("(p t) o -> p (t o)", t=PACK))
@@ -113,57 +118,62 @@ def tile_picked_twlpullblerp_none_po_kernel(
 
         two_codes = keep.tile([P, S], U32, align_bytes=64)
         two_scales = keep.tile([P, S], U8, align_bytes=64)
-        idx_codes = keep.tile([P, S], U32, align_bytes=64)
         idx_scales = keep.tile([P, S], U8, align_bytes=64)
 
-        deal_words(nc.vector, w_words[1], w2_raw)
+        deal_words(nc.gpsimd, w_words[1], w2_raw)
+        deal_words(nc.gpsimd, w_words[0], w1_raw)
+        deal_words(nc.gpsimd, w_words[2], w3_raw)
+        (lo0, hi0), (lo1, hi1) = HALVES
         nc.vector.tensor_copy(two_codes[:], x_table[:].bitcast(U32).indirect(two_l[:]))
         nc.vector.tensor_copy(two_scales[:], x_plane[:].indirect(two_l[:]))
-        deal_plane(nc.vector, w_planes[1], raw_planes[1])
+        deal_plane(nc.vector, w_planes[1], w2_raw_plane)
+        idx_codes = keep.tile([P, S], U32, tag="after_w2_plane", align_bytes=64)
         nc.vector.tensor_copy(idx_codes[:], x_table[:].bitcast(U32).indirect(offs_l[:]))
         nc.vector.tensor_copy(idx_scales[:], x_plane[:].indirect(offs_l[:]))
-        deal_words(nc.vector, w_words[0], w1_raw)
-        deal_plane(nc.vector, w_planes[0], raw_planes[0])
-        nc.sync.dma_start(out=w2_raw[:].bitcast(I32), in_=w3_words[0].bitcast(I32))
-        load_scale_rows(nc.sync, raw_planes[1], w3_scales)
+        deal_plane(nc.vector, w_planes[0], raw_plane)
+        load_scale_rows(nc.sync, raw_plane, w3_scales)
 
-        d_acc = [psum.tile([P, S], F32, name="d_acc%d" % t, tag="bank%d" % t) for t in range(PACK)]
-        y_acc = [psum.tile([P, S], F32, name="y_acc%d" % t, tag="bank%d" % (PACK + t)) for t in range(PACK)]
-        for t in range(PACK):
-            product(nc, d_acc[t][:], w_words[1], w_planes[1], t, two_codes[:], two_scales[:])
-        for t in range(PACK):
-            product(nc, y_acc[t][:], w_words[0], w_planes[0], t, idx_codes[:], idx_scales[:])
-
-        d_rows = [keep.tile([P, S], F32, name="d_rows%d" % t) for t in range(PACK)]
-        d_here = [keep.tile([P, S], F32, name="d_here%d" % t) for t in range(PACK)]
-        gy_rows = [keep.tile([P, S], F32, name="gy_rows%d" % t) for t in range(PACK)]
-        diff = [keep.tile([P, S], F32, name="diff%d" % t) for t in range(PACK)]
+        d_rows = [keep.tile([P, S if t == 0 else 2 * S], F32, name="d_rows%d" % t) for t in range(PACK)]
+        d_last = keep.tile([P, S], F32)
+        d_here = [d_rows[t + 1][:, S:] for t in range(PACK - 1)] + [d_last[:]]
+        gy_rows = [keep.tile([P, 2 * S], F32, name="gy_rows%d" % t) for t in range(PACK)]
+        diff = [gy_rows[t][:, S:] for t in range(PACK)]
         pull = [keep.tile([P, S], F32, name="pull%d" % t) for t in range(PACK)]
         far = keep.tile([P, PACK, S], F32)
         near = keep.tile([P, PACK, S], F32)
 
+        d_parts = []
+        for t in range(PACK):
+            parts = []
+            for lo, hi in HALVES if t == 0 else [(0, S)]:
+                acc = psum.tile([P, hi - lo], F32, name="d_acc%d_%d" % (t, lo), tag="bank%d" % (7 if lo else t))
+                product(nc, acc[:], w_words[1], w_planes[1], t, two_codes[:, lo:hi], two_scales[:, lo:hi])
+                parts.append((acc, lo, hi))
+            d_parts.append(parts)
+
         def gate_input(t):
-            nc.scalar.copy(d_rows[t][:], d_acc[t][:])
-            nc.scalar.copy(d_here[t][:], d_acc[t][:])
-            for lo, hi in HALVES:
+            for acc, lo, hi in d_parts[t]:
+                nc.scalar.copy(d_rows[t][:, lo:hi], acc[:])
+                nc.scalar.copy(d_here[t][:, lo:hi], acc[:])
+            for acc, lo, hi in d_parts[t]:
                 nc.vector.tensor_tensor(diff[t][:, lo:hi], d_rows[t][:].indirect(entries(n2_l, lo, hi)), d_here[t][:, lo:hi], ALU.subtract)
 
         def blend_terms(t):
-            nc.scalar.activation(gy_rows[t][:], y_acc[t][:], ACT.Copy, scale=gain[:, t : t + 1])
-            nc.scalar.activation(pull[t][:], diff[t][:], ACT.Sigmoid)
-            for lo, hi in HALVES:
-                nc.vector.tensor_tensor(far[:, t, lo:hi], gy_rows[t][:].indirect(entries(n1_l, lo, hi)), pull[t][:, lo:hi], ALU.mult)
-            nc.vector.scalar_tensor_tensor(near[:, t, :], pull[t][:], 1.0, gy_rows[t][:], ALU.subtract, ALU.mult)
+            y_acc = psum.tile([P, S], F32, name="y_acc%d" % t, tag="bank%d" % ((PACK + t) % 7))
+            product(nc, y_acc[:], w_words[0], w_planes[0], t, idx_codes[:], idx_scales[:])
+            nc.scalar.activation(pull[t][:], diff[t], ACT.Sigmoid)
+            nc.scalar.activation(gy_rows[t][:, :S], y_acc[:], ACT.Copy, scale=gain[:, t : t + 1])
+            nc.vector.tensor_tensor(far[:, t, :], gy_rows[t][:].indirect(n1_l[:]), pull[t][:], ALU.mult)
+            nc.vector.scalar_tensor_tensor(near[:, t, :], pull[t][:], 1.0, gy_rows[t][:, :S], ALU.subtract, ALU.mult)
 
         gate_input(0)
         for t in range(PACK):
             if t + 1 < PACK:
                 gate_input(t + 1)
             blend_terms(t)
-        deal_words(nc.vector, w_words[2], w2_raw)
-        deal_plane(nc.vector, w_planes[2], raw_planes[1])
+        deal_plane(nc.vector, w_planes[2], raw_plane)
 
-        h_acc = [psum.tile([P, S], F32, name="h_acc%d" % t, tag="bank%d" % t) for t in range(PACK)]
+        h_acc = [psum.tile([P, S], F32, name="h_acc%d" % t, tag="bank%d" % (t + 1)) for t in range(PACK)]
         h_rows = [keep.tile([P, S], F32, name="h_rows%d" % t) for t in range(PACK)]
         z_woven = [keep.tile([P, PACK * (hi - lo)], BF16, name="z_woven%d" % lo, align_bytes=64) for lo, hi in Z_PIECES]
         z_codes = [keep.tile([P, hi - lo], U32, name="z_codes%d" % lo, align_bytes=64) for lo, hi in Z_PIECES]
@@ -192,34 +202,56 @@ def tile_picked_twlpullblerp_none_po_kernel(
         out_rows = out_0.rearrange("(p t) j -> p t j", t=PACK)
         out_words = out_1[0].rearrange("p j r -> p (j r)").bitcast(I32)
         o_scales = keep.tile([P, S], U8, align_bytes=64)
-        for lo, hi in OUT_PIECES:
-            w = hi - lo
-            result = keep.tile([P, PACK, w], F32, name="result%d" % lo)
-            for t in range(PACK):
-                mix = keep.tile([P, w], F32, name="mix%d_%d" % (lo, t))
-                rest = keep.tile([P, w], F32, name="rest%d_%d" % (lo, t))
-                term5 = keep.tile([P, w], F32, name="term5_%d_%d" % (lo, t))
-                term3 = keep.tile([P, w], F32, name="term3_%d_%d" % (lo, t))
-                nc.scalar.activation(mix[:], h_rows[t][:].indirect(entries(n4_l, lo, hi)), ACT.Sigmoid)
-                if lo == 0 and t == 0:
-                    nc.vector.tensor_copy(term3[:], h_rows[t][:].indirect(entries(n3_l, lo, hi)))
-                    nc.vector.tensor_tensor(rest[:], h_rows[t][:].indirect(entries(n5_l, lo, hi)), term3[:], ALU.subtract)
-                    nc.vector.tensor_tensor(term5[:], rest[:], mix[:], ALU.mult)
-                    nc.vector.tensor_tensor(result[:, t, :], term3[:], term5[:], ALU.add)
-                    continue
-                nc.scalar.activation(rest[:], mix[:], ACT.Copy, scale=-1.0, bias=1.0)
-                nc.vector.tensor_tensor(term5[:], h_rows[t][:].indirect(entries(n5_l, lo, hi)), mix[:], ALU.mult)
-                nc.vector.tensor_tensor(term3[:], h_rows[t][:].indirect(entries(n3_l, lo, hi)), rest[:], ALU.mult)
-                nc.vector.tensor_tensor(result[:, t, :], term3[:], term5[:], ALU.add)
-            nc.sync.dma_start(out=out_rows[:, :, lo:hi], in_=result[:])
-            o_woven = keep.tile([P, PACK * w], BF16, name="o_woven%d" % lo, align_bytes=64)
-            if hi < S:
-                nc.scalar.copy(woven(o_woven), by_pairs(result[:]))
+        o_codes = [keep.tile([P, hi - lo], U32, name="o_codes%d" % lo, align_bytes=64) for lo, hi in HALVES]
+        mix = keep.tile([P, PACK, S], F32)
+        rest = keep.tile([P, PACK, S], F32)
+        term3 = keep.tile([P, PACK, S], F32)
+        term5 = keep.tile([P, PACK, S], F32)
+        result = keep.tile([P, PACK, S], F32)
+
+        def terms(t, lo, hi):
+            nc.scalar.activation(mix[:, t, lo:hi], h_rows[t][:].indirect(entries(n4_l, lo, hi)), ACT.Sigmoid)
+            if lo == 0 and t == 0:
+                nc.vector.tensor_copy(term3[:, t, lo:hi], h_rows[t][:].indirect(entries(n3_l, lo, hi)))
+                nc.vector.tensor_tensor(rest[:, t, lo:hi], h_rows[t][:].indirect(entries(n5_l, lo, hi)), term3[:, t, lo:hi], ALU.subtract)
+                nc.vector.tensor_tensor(term5[:, t, lo:hi], rest[:, t, lo:hi], mix[:, t, lo:hi], ALU.mult)
             else:
-                nc.vector.tensor_copy(woven(o_woven), by_pairs(result[:]))
-            o_codes = keep.tile([P, w], U32, name="o_codes%d" % lo, align_bytes=64)
-            nc.vector.quantize_mx(out=o_codes[:].bitcast(FP8X4), scales=o_scales[:, lo:hi], in_=o_woven[:])
-            nc.sync.dma_start(out=out_words[:, lo:hi], in_=o_codes[:].bitcast(I32))
+                nc.scalar.activation(rest[:, t, lo:hi], mix[:, t, lo:hi], ACT.Copy, scale=-1.0, bias=1.0)
+                nc.vector.tensor_tensor(term5[:, t, lo:hi], h_rows[t][:].indirect(entries(n5_l, lo, hi)), mix[:, t, lo:hi], ALU.mult)
+                nc.vector.tensor_tensor(term3[:, t, lo:hi], h_rows[t][:].indirect(entries(n3_l, lo, hi)), rest[:, t, lo:hi], ALU.mult)
+
+        def add_terms(t0, t1, lo, hi):
+            nc.vector.tensor_tensor(result[:, t0:t1, lo:hi], term3[:, t0:t1, lo:hi], term5[:, t0:t1, lo:hi], ALU.add)
+
+        def store_rows(t0, t1, lo, hi):
+            nc.sync.dma_start(out=out_rows[:, t0:t1, lo:hi], in_=result[:, t0:t1, lo:hi])
+
+        def planes(lo, hi):
+            o_woven = keep.tile([P, PACK * (hi - lo)], BF16, name="o_woven%d" % lo, align_bytes=64)
+            if hi < S:
+                nc.scalar.copy(woven(o_woven), by_pairs(result[:, :, lo:hi]))
+            else:
+                nc.vector.tensor_copy(woven(o_woven), by_pairs(result[:, :, lo:hi]))
+            codes = o_codes[lo // lo1][:, lo % lo1 : lo % lo1 + hi - lo]
+            nc.vector.quantize_mx(out=codes.bitcast(FP8X4), scales=o_scales[:, lo:hi], in_=o_woven[:])
+
+        for t in range(PACK):
+            terms(t, lo0, hi0)
+        add_terms(0, PACK, lo0, hi0)
+        store_rows(0, PACK, lo0, hi0)
+        for t in range(PACK - 1):
+            terms(t, lo1, hi1)
+        planes(lo0, hi0)
+        nc.sync.dma_start(out=out_words[:, lo0:hi0], in_=o_codes[0][:].bitcast(I32))
+        add_terms(0, PACK - 1, lo1, hi1)
+        store_rows(0, PACK - 1, lo1, hi1)
+        for lo, hi in OUT_PIECES[1:]:
+            terms(PACK - 1, lo, hi)
+            add_terms(PACK - 1, PACK, lo, hi)
+        store_rows(PACK - 1, PACK, lo1, hi1)
+        for lo, hi in OUT_PIECES[1:]:
+            planes(lo, hi)
+        nc.sync.dma_start(out=out_words[:, lo1:hi1], in_=o_codes[1][:].bitcast(I32))
         for q in range(4):
             queue = nc.scalar if q % 2 else nc.sync
             queue.dma_start(out=out_2[0, 4 * q : 4 * q + 4, :].bitcast(I32), in_=o_scales[32 * q : 32 * q + 4, :].bitcast(I32))

@@ -34,8 +34,8 @@ def load_scale_rows(queue, plane, scales):
 
 def deal_words(eng, words, raw_words):
     eng.tensor_copy(
-        out=words[:].rearrange("p (t m b) -> p t m b", t=PACK, b=2),
-        in_=raw_words[:].rearrange("p (m t b) -> p t m b", t=PACK, b=2),
+        out=words[:].bitcast(U16).rearrange("p (t m) -> p t m", t=PACK),
+        in_=raw_words[:].bitcast(U16).rearrange("p (m t) -> p t m", t=PACK),
     )
 
 
@@ -87,7 +87,8 @@ def tile_picked_twlpullblerp_none_po_kernel(
 
         x_plane = keep.tile([P, T], U8, align_bytes=64)
         nc.vector.memset(x_plane[:].bitcast(I32), 0)
-        w2_raw_plane = keep.tile([P, H], U8, tag="after_w2_plane", align_bytes=64)
+        shared = ctx.enter_context(tc.tile_pool(name="shared", bufs=1))
+        w2_raw_plane = shared.tile([P, H], U8, offset=768, align_bytes=64)
         nc.vector.memset(w2_raw_plane[:].bitcast(I32), 0)
         raw_plane = keep.tile([P, H], U8, align_bytes=64)
         nc.vector.memset(raw_plane[:].bitcast(I32), 0)
@@ -96,15 +97,15 @@ def tile_picked_twlpullblerp_none_po_kernel(
         nc.scalar.activation(warm[:, 1:2], warm[:, 0:1], ACT.Sigmoid)
 
         load_scale_rows(nc.sync, x_plane, x_scales)
-        x_table = keep.tile([P, T], I32, align_bytes=64)
-        two_l = load_list(two, "two_l")
         w2_raw = load_words(w2_words, "w2_raw")
+        two_l = load_list(two, "two_l")
+        w1_raw = load_words(w1_words, "w1_raw")
+        w3_raw = load_words(w3_words, "w3_raw")
         offs_l = load_list(offs, "offs_l")
+        x_table = keep.tile([P, T], I32, align_bytes=64)
         nc.sync.dma_start(out=x_table[:], in_=x_words[0].rearrange("p n t -> p (n t)").bitcast(I32))
         load_scale_rows(nc.sync, w2_raw_plane, w2_scales)
-        w1_raw = load_words(w1_words, "w1_raw")
         load_scale_rows(nc.sync, raw_plane, w1_scales)
-        w3_raw = load_words(w3_words, "w3_raw")
         n2_l = load_list(n2, "n2_l")
         gain = keep.tile([P, PACK], F32)
         nc.sync.dma_start(out=gain[:], in_=gn.rearrange("(p t) o -> p (t o)", t=PACK))
@@ -116,20 +117,22 @@ def tile_picked_twlpullblerp_none_po_kernel(
         w_words = [keep.tile([P, 2 * H], U8, name="w_words%d" % i, align_bytes=64) for i in range(3)]
         w_planes = [keep.tile([P, H], U8, name="w_plane%d" % i, align_bytes=64) for i in range(3)]
 
-        two_codes = keep.tile([P, S], U32, align_bytes=64)
         two_scales = keep.tile([P, S], U8, align_bytes=64)
         idx_scales = keep.tile([P, S], U8, align_bytes=64)
 
-        deal_words(nc.gpsimd, w_words[1], w2_raw)
-        deal_words(nc.gpsimd, w_words[0], w1_raw)
-        deal_words(nc.gpsimd, w_words[2], w3_raw)
-        (lo0, hi0), (lo1, hi1) = HALVES
-        nc.vector.tensor_copy(two_codes[:], x_table[:].bitcast(U32).indirect(two_l[:]))
+        deal_words(nc.vector, w_words[1], w2_raw)
+        deal_words(nc.vector, w_words[0], w1_raw)
+        deal_words(nc.vector, w_words[2], w3_raw)
         nc.vector.tensor_copy(two_scales[:], x_plane[:].indirect(two_l[:]))
-        deal_plane(nc.vector, w_planes[1], w2_raw_plane)
-        idx_codes = keep.tile([P, S], U32, tag="after_w2_plane", align_bytes=64)
-        nc.vector.tensor_copy(idx_codes[:], x_table[:].bitcast(U32).indirect(offs_l[:]))
         nc.vector.tensor_copy(idx_scales[:], x_plane[:].indirect(offs_l[:]))
+        two_codes = {}
+        for lo, hi in HALVES:
+            two_codes[lo] = shared.tile([P, hi - lo], U32, name="two_codes%d" % lo, offset=0 if lo else 3072, align_bytes=64)
+            nc.vector.tensor_copy(two_codes[lo][:], x_table[:].bitcast(U32).indirect(entries(two_l, lo, hi)))
+            if lo == 0:
+                deal_plane(nc.vector, w_planes[1], w2_raw_plane)
+        idx_codes = shared.tile([P, S], U32, offset=1024, align_bytes=64)
+        nc.vector.tensor_copy(idx_codes[:], x_table[:].bitcast(U32).indirect(offs_l[:]))
         deal_plane(nc.vector, w_planes[0], raw_plane)
         load_scale_rows(nc.sync, raw_plane, w3_scales)
 
@@ -144,11 +147,15 @@ def tile_picked_twlpullblerp_none_po_kernel(
 
         d_parts = []
         for t in range(PACK):
-            parts = []
-            for lo, hi in HALVES if t == 0 else [(0, S)]:
-                acc = psum.tile([P, hi - lo], F32, name="d_acc%d_%d" % (t, lo), tag="bank%d" % (7 if lo else t))
-                product(nc, acc[:], w_words[1], w_planes[1], t, two_codes[:, lo:hi], two_scales[:, lo:hi])
-                parts.append((acc, lo, hi))
+            if t == 0:
+                parts = [(psum.tile([P, hi - lo], F32, name="d_acc0_%d" % lo, tag="bank%d" % (7 if lo else 0)), lo, hi) for lo, hi in HALVES]
+                for acc, lo, hi in parts:
+                    product(nc, acc[:], w_words[1], w_planes[1], t, two_codes[lo][:], two_scales[:, lo:hi])
+            else:
+                acc = psum.tile([P, S], F32, name="d_acc%d" % t, tag="bank%d" % t)
+                parts = [(acc, 0, S)]
+                for lo, hi in HALVES:
+                    product(nc, acc[:, lo:hi], w_words[1], w_planes[1], t, two_codes[lo][:], two_scales[:, lo:hi])
             d_parts.append(parts)
 
         def gate_input(t):
@@ -174,7 +181,7 @@ def tile_picked_twlpullblerp_none_po_kernel(
         deal_plane(nc.vector, w_planes[2], raw_plane)
 
         h_acc = [psum.tile([P, S], F32, name="h_acc%d" % t, tag="bank%d" % (t + 1)) for t in range(PACK)]
-        h_rows = [keep.tile([P, S], F32, name="h_rows%d" % t) for t in range(PACK)]
+        h_rows = d_rows[1:] + d_rows[:1]
         z_woven = [keep.tile([P, PACK * (hi - lo)], BF16, name="z_woven%d" % lo, align_bytes=64) for lo, hi in Z_PIECES]
         z_codes = [keep.tile([P, hi - lo], U32, name="z_codes%d" % lo, align_bytes=64) for lo, hi in Z_PIECES]
         z_scales = [keep.tile([P, hi - lo], U8, name="z_scales%d" % lo, align_bytes=64) for lo, hi in Z_PIECES]
@@ -202,7 +209,7 @@ def tile_picked_twlpullblerp_none_po_kernel(
         out_rows = out_0.rearrange("(p t) j -> p t j", t=PACK)
         out_words = out_1[0].rearrange("p j r -> p (j r)").bitcast(I32)
         o_scales = keep.tile([P, S], U8, align_bytes=64)
-        o_codes = [keep.tile([P, hi - lo], U32, name="o_codes%d" % lo, align_bytes=64) for lo, hi in HALVES]
+        o_codes = keep.tile([P, S], U32, align_bytes=64)
         mix = keep.tile([P, PACK, S], F32)
         rest = keep.tile([P, PACK, S], F32)
         term3 = keep.tile([P, PACK, S], F32)
@@ -232,26 +239,28 @@ def tile_picked_twlpullblerp_none_po_kernel(
                 nc.scalar.copy(woven(o_woven), by_pairs(result[:, :, lo:hi]))
             else:
                 nc.vector.tensor_copy(woven(o_woven), by_pairs(result[:, :, lo:hi]))
-            codes = o_codes[lo // lo1][:, lo % lo1 : lo % lo1 + hi - lo]
-            nc.vector.quantize_mx(out=codes.bitcast(FP8X4), scales=o_scales[:, lo:hi], in_=o_woven[:])
+            nc.vector.quantize_mx(out=o_codes[:, lo:hi].bitcast(FP8X4), scales=o_scales[:, lo:hi], in_=o_woven[:])
 
-        for t in range(PACK):
-            terms(t, lo0, hi0)
+        (lo0, hi0), (lo1, hi1) = HALVES
+        for lo, hi in HALVES:
+            terms(0, lo, hi)
+        terms(1, 0, S)
+        terms(2, lo0, hi0)
+        terms(3, lo0, hi0)
         add_terms(0, PACK, lo0, hi0)
         store_rows(0, PACK, lo0, hi0)
-        for t in range(PACK - 1):
-            terms(t, lo1, hi1)
-        planes(lo0, hi0)
-        nc.sync.dma_start(out=out_words[:, lo0:hi0], in_=o_codes[0][:].bitcast(I32))
+        terms(2, lo1, hi1)
         add_terms(0, PACK - 1, lo1, hi1)
         store_rows(0, PACK - 1, lo1, hi1)
+        planes(lo0, hi0)
+        nc.sync.dma_start(out=out_words[:, lo0:hi0], in_=o_codes[:, lo0:hi0].bitcast(I32))
         for lo, hi in OUT_PIECES[1:]:
             terms(PACK - 1, lo, hi)
             add_terms(PACK - 1, PACK, lo, hi)
         store_rows(PACK - 1, PACK, lo1, hi1)
         for lo, hi in OUT_PIECES[1:]:
             planes(lo, hi)
-        nc.sync.dma_start(out=out_words[:, lo1:hi1], in_=o_codes[1][:].bitcast(I32))
+        nc.sync.dma_start(out=out_words[:, lo1:hi1], in_=o_codes[:, lo1:hi1].bitcast(I32))
         for q in range(4):
             queue = nc.scalar if q % 2 else nc.sync
             queue.dma_start(out=out_2[0, 4 * q : 4 * q + 4, :].bitcast(I32), in_=o_scales[32 * q : 32 * q + 4, :].bitcast(I32))

@@ -1,6 +1,7 @@
 from contextlib import ExitStack
 
 import concourse.mybir as mybir
+from concourse.masks import make_identity
 
 K, T, S, H, N = 512, 2048, 512, 512, 512
 FLOPS = 2 * K * H * S * 2 + 2 * H * N * S
@@ -95,6 +96,9 @@ def tile_picked_twlpullblerp_none_po_kernel(
         warm = keep.tile([P, 2], F32)
         nc.gpsimd.memset(warm[:, 0:1], 0.0)
         nc.scalar.activation(warm[:, 1:2], warm[:, 0:1], ACT.Sigmoid)
+
+        ident = keep.tile([P, P], F32)
+        make_identity(nc, ident[:])
 
         load_scale_rows(nc.sync, x_plane, x_scales)
         w2_raw = load_words(w2_words, "w2_raw")
@@ -195,9 +199,7 @@ def tile_picked_twlpullblerp_none_po_kernel(
             nc.vector.quantize_mx(out=z_codes[i][:].bitcast(FP8X4), scales=z_scales[i][:], in_=z_woven[i][:])
             for t in range(PACK):
                 product(nc, h_acc[t][:, lo:hi], w_words[2], w_planes[2], t, z_codes[i][:], z_scales[i][:])
-                if hi == S and t == 0:
-                    nc.vector.tensor_copy(h_rows[t][:, lo:hi], h_acc[t][:, lo:hi])
-                else:
+                if hi < S:
                     nc.scalar.copy(h_rows[t][:, lo:hi], h_acc[t][:, lo:hi])
 
         blend(0)
@@ -216,19 +218,34 @@ def tile_picked_twlpullblerp_none_po_kernel(
         term5 = keep.tile([P, PACK, S], F32)
         result = keep.tile([P, PACK, S], F32)
 
-        def terms(t, lo, hi):
+        def weights(t, lo, hi):
             nc.scalar.activation(mix[:, t, lo:hi], h_rows[t][:].indirect(entries(n4_l, lo, hi)), ACT.Sigmoid)
+            if lo or t:
+                nc.scalar.activation(rest[:, t, lo:hi], mix[:, t, lo:hi], ACT.Copy, scale=-1.0, bias=1.0)
+
+        def terms(t, lo, hi):
             if lo == 0 and t == 0:
                 nc.vector.tensor_copy(term3[:, t, lo:hi], h_rows[t][:].indirect(entries(n3_l, lo, hi)))
                 nc.vector.tensor_tensor(rest[:, t, lo:hi], h_rows[t][:].indirect(entries(n5_l, lo, hi)), term3[:, t, lo:hi], ALU.subtract)
                 nc.vector.tensor_tensor(term5[:, t, lo:hi], rest[:, t, lo:hi], mix[:, t, lo:hi], ALU.mult)
             else:
-                nc.scalar.activation(rest[:, t, lo:hi], mix[:, t, lo:hi], ACT.Copy, scale=-1.0, bias=1.0)
                 nc.vector.tensor_tensor(term5[:, t, lo:hi], h_rows[t][:].indirect(entries(n5_l, lo, hi)), mix[:, t, lo:hi], ALU.mult)
                 nc.vector.tensor_tensor(term3[:, t, lo:hi], h_rows[t][:].indirect(entries(n3_l, lo, hi)), rest[:, t, lo:hi], ALU.mult)
 
         def add_terms(t0, t1, lo, hi):
             nc.vector.tensor_tensor(result[:, t0:t1, lo:hi], term3[:, t0:t1, lo:hi], term5[:, t0:t1, lo:hi], ALU.add)
+
+        def add_terms_on_tensor(t):
+            turned_sum = psum.tile([P, S], F32, name="turned_sum%d" % t, tag="bank%d" % (5 + t))
+            for lo in range(0, S, P):
+                nc.tensor.matmul(turned_sum[:, lo : lo + P], term5[:, t, lo : lo + P], ident[:], start=True, stop=False, is_transpose=True)
+                nc.tensor.matmul(turned_sum[:, lo : lo + P], term3[:, t, lo : lo + P], ident[:], start=False, stop=True, is_transpose=True)
+            turned = keep.tile([P, S], F32, name="turned%d" % t)
+            nc.scalar.copy(turned[:], turned_sum[:])
+            back = psum.tile([P, S], F32, name="back%d" % t, tag="bank%d" % (7 * t))
+            for lo in range(0, S, P):
+                nc.tensor.transpose(back[:, lo : lo + P], turned[:, lo : lo + P], ident[:])
+            nc.scalar.copy(result[:, t, :], back[:])
 
         def store_rows(t0, t1, lo, hi):
             nc.sync.dma_start(out=out_rows[:, t0:t1, lo:hi], in_=result[:, t0:t1, lo:hi])
@@ -241,26 +258,32 @@ def tile_picked_twlpullblerp_none_po_kernel(
                 nc.vector.tensor_copy(woven(o_woven), by_pairs(result[:, :, lo:hi]))
             nc.vector.quantize_mx(out=o_codes[:, lo:hi].bitcast(FP8X4), scales=o_scales[:, lo:hi], in_=o_woven[:])
 
-        (lo0, hi0), (lo1, hi1) = HALVES
+        last_lo = Z_PIECES[-1][0]
+        for t in range(PACK):
+            if t == 0:
+                nc.vector.tensor_copy(h_rows[t][:, last_lo:S], h_acc[t][:, last_lo:S])
+            else:
+                nc.scalar.copy(h_rows[t][:, last_lo:S], h_acc[t][:, last_lo:S])
+            for lo, hi in HALVES if t in (0, PACK - 1) else [(0, S)]:
+                weights(t, lo, hi)
         for lo, hi in HALVES:
             terms(0, lo, hi)
-        terms(1, 0, S)
-        terms(2, lo0, hi0)
-        terms(3, lo0, hi0)
-        add_terms(0, PACK, lo0, hi0)
-        store_rows(0, PACK, lo0, hi0)
-        terms(2, lo1, hi1)
-        add_terms(0, PACK - 1, lo1, hi1)
-        store_rows(0, PACK - 1, lo1, hi1)
-        planes(lo0, hi0)
-        nc.sync.dma_start(out=out_words[:, lo0:hi0], in_=o_codes[:, lo0:hi0].bitcast(I32))
+        for t in range(1, PACK - 1):
+            terms(t, 0, S)
+        terms(PACK - 1, *OUT_PIECES[0])
+        add_terms_on_tensor(0)
+        add_terms_on_tensor(1)
+        store_rows(0, 2, 0, S)
+        add_terms(2, PACK - 1, 0, S)
+        store_rows(2, PACK - 1, 0, S)
+        add_terms(PACK - 1, PACK, *OUT_PIECES[0])
         for lo, hi in OUT_PIECES[1:]:
             terms(PACK - 1, lo, hi)
             add_terms(PACK - 1, PACK, lo, hi)
-        store_rows(PACK - 1, PACK, lo1, hi1)
-        for lo, hi in OUT_PIECES[1:]:
+        store_rows(PACK - 1, PACK, 0, S)
+        for lo, hi in OUT_PIECES:
             planes(lo, hi)
-        nc.sync.dma_start(out=out_words[:, lo1:hi1], in_=o_codes[:, lo1:hi1].bitcast(I32))
+        nc.sync.dma_start(out=out_words, in_=o_codes[:].bitcast(I32))
         for q in range(4):
             queue = nc.scalar if q % 2 else nc.sync
             queue.dma_start(out=out_2[0, 4 * q : 4 * q + 4, :].bitcast(I32), in_=o_scales[32 * q : 32 * q + 4, :].bitcast(I32))

from contextlib import ExitStack

import concourse.mybir as mybir
from concourse.masks import make_identity

K, T, S, H, N = 512, 2048, 512, 512, 512
FLOPS = 2 * K * H * S * 2 + 2 * H * N * S

F32 = mybir.dt.float32
BF16 = mybir.dt.bfloat16
I32 = mybir.dt.int32
U32 = mybir.dt.uint32
U16 = mybir.dt.uint16
U8 = mybir.dt.uint8
FP8X4 = mybir.dt.float8_e4m3fn_x4
FP4X4 = mybir.dt.float4_e2m1fn_x4
ALU = mybir.AluOpType
ACT = mybir.ActivationFunctionType

P = 128
PACK = 4
HALVES = [(0, 256), (256, 512)]
Z_PIECES = [(0, 256), (256, 384), (384, 512)]
OUT_PIECES = [(0, 256), (256, 384), (384, 512)]


def entries(list_tile, lo, hi):
    return list_tile[:, lo // 16 : hi // 16]


def load_scale_rows(queue, plane, scales):
    for q in range(4):
        queue.dma_start(out=plane[32 * q : 32 * q + 4, :].bitcast(I32), in_=scales[0, 4 * q : 4 * q + 4, :].bitcast(I32))


def deal_words(eng, words, raw_words):
    eng.tensor_copy(
        out=words[:].bitcast(U16).rearrange("p (t m) -> p t m", t=PACK),
        in_=raw_words[:].bitcast(U16).rearrange("p (m t) -> p t m", t=PACK),
    )


def deal_plane(eng, plane, raw_plane):
    eng.tensor_copy(
        out=plane[:].rearrange("p (t m) -> p t m", t=PACK),
        in_=raw_plane[:].rearrange("p (m t) -> p t m", t=PACK),
    )


def product(nc, acc, words, plane, t, codes, scales):
    nc.tensor.matmul_mx(
        out=acc,
        lhsT=words[:, 2 * P * t : 2 * P * (t + 1)].bitcast(FP4X4),
        lhsT_scale=plane[:, P * t : P * (t + 1)],
        rhs=codes.bitcast(FP8X4),
        rhs_scale=scales,
        start=True,
        stop=True,
    )


def woven(tile):
    return tile[:].rearrange("p (c i t) -> p c t i", t=PACK, i=2)


def by_pairs(ap):
    return ap.rearrange("p t (c i) -> p c t i", i=2)


def tile_picked_twlpullblerp_none_po_kernel(
    tc, x_words, x_scales, w1_words, w1_scales, w2_words, w2_scales, gn, w3_words, w3_scales,
    offs, two, n1, n2, n3, n4, n5, out_0, out_1, out_2,
):
    nc = tc.nc
    with ExitStack() as ctx:
        keep = ctx.enter_context(tc.tile_pool(name="keep", bufs=1))
        psum = ctx.enter_context(tc.psum_pool(name="psum", bufs=1))

        def load_list(src, name):
            lst = keep.tile([P, S // 16], U16, name=name)
            nc.sync.dma_start(lst[:], src)
            return lst

        def load_words(src, name):
            raw = keep.tile([P, 2 * H], U8, name=name, align_bytes=64)
            nc.sync.dma_start(out=raw[:].bitcast(I32), in_=src[0].bitcast(I32))
            return raw

        x_plane = keep.tile([P, T], U8, align_bytes=64)
        nc.vector.memset(x_plane[:].bitcast(I32), 0)
        shared = ctx.enter_context(tc.tile_pool(name="shared", bufs=1))
        w2_raw_plane = shared.tile([P, H], U8, offset=768, align_bytes=64)
        nc.vector.memset(w2_raw_plane[:].bitcast(I32), 0)
        raw_plane = keep.tile([P, H], U8, align_bytes=64)
        nc.vector.memset(raw_plane[:].bitcast(I32), 0)
        warm = keep.tile([P, 2], F32)
        nc.gpsimd.memset(warm[:, 0:1], 0.0)
        nc.scalar.activation(warm[:, 1:2], warm[:, 0:1], ACT.Sigmoid)

        ident = keep.tile([P, P], F32)
        make_identity(nc, ident[:])

        load_scale_rows(nc.sync, x_plane, x_scales)
        w2_raw = load_words(w2_words, "w2_raw")
        two_l = load_list(two, "two_l")
        w1_raw = load_words(w1_words, "w1_raw")
        w3_raw = load_words(w3_words, "w3_raw")
        offs_l = load_list(offs, "offs_l")
        x_table = keep.tile([P, T], I32, align_bytes=64)
        nc.sync.dma_start(out=x_table[:], in_=x_words[0].rearrange("p n t -> p (n t)").bitcast(I32))
        load_scale_rows(nc.sync, w2_raw_plane, w2_scales)
        load_scale_rows(nc.sync, raw_plane, w1_scales)
        n2_l = load_list(n2, "n2_l")
        gain = keep.tile([P, PACK], F32)
        nc.sync.dma_start(out=gain[:], in_=gn.rearrange("(p t) o -> p (t o)", t=PACK))
        n1_l = load_list(n1, "n1_l")
        n4_l = load_list(n4, "n4_l")
        n3_l = load_list(n3, "n3_l")
        n5_l = load_list(n5, "n5_l")

        w_words = [keep.tile([P, 2 * H], U8, name="w_words%d" % i, align_bytes=64) for i in range(3)]
        w_planes = [keep.tile([P, H], U8, name="w_plane%d" % i, align_bytes=64) for i in range(3)]

        two_scales = keep.tile([P, S], U8, align_bytes=64)
        idx_scales = keep.tile([P, S], U8, align_bytes=64)

        deal_words(nc.vector, w_words[1], w2_raw)
        deal_words(nc.vector, w_words[0], w1_raw)
        deal_words(nc.vector, w_words[2], w3_raw)
        nc.vector.tensor_copy(two_scales[:], x_plane[:].indirect(two_l[:]))
        nc.vector.tensor_copy(idx_scales[:], x_plane[:].indirect(offs_l[:]))
        two_codes = {}
        for lo, hi in HALVES:
            two_codes[lo] = shared.tile([P, hi - lo], U32, name="two_codes%d" % lo, offset=0 if lo else 3072, align_bytes=64)
            nc.vector.tensor_copy(two_codes[lo][:], x_table[:].bitcast(U32).indirect(entries(two_l, lo, hi)))
            if lo == 0:
                deal_plane(nc.vector, w_planes[1], w2_raw_plane)
        idx_codes = shared.tile([P, S], U32, offset=1024, align_bytes=64)
        nc.vector.tensor_copy(idx_codes[:], x_table[:].bitcast(U32).indirect(offs_l[:]))
        deal_plane(nc.vector, w_planes[0], raw_plane)
        load_scale_rows(nc.sync, raw_plane, w3_scales)

        d_rows = [keep.tile([P, S if t == 0 else 2 * S], F32, name="d_rows%d" % t) for t in range(PACK)]
        d_last = keep.tile([P, S], F32)
        d_here = [d_rows[t + 1][:, S:] for t in range(PACK - 1)] + [d_last[:]]
        gy_rows = [keep.tile([P, 2 * S], F32, name="gy_rows%d" % t) for t in range(PACK)]
        diff = [gy_rows[t][:, S:] for t in range(PACK)]
        pull = [keep.tile([P, S], F32, name="pull%d" % t) for t in range(PACK)]
        far = keep.tile([P, PACK, S], F32)
        near = keep.tile([P, PACK, S], F32)

        d_parts = []
        for t in range(PACK):
            if t == 0:
                parts = [(psum.tile([P, hi - lo], F32, name="d_acc0_%d" % lo, tag="bank%d" % (7 if lo else 0)), lo, hi) for lo, hi in HALVES]
                for acc, lo, hi in parts:
                    product(nc, acc[:], w_words[1], w_planes[1], t, two_codes[lo][:], two_scales[:, lo:hi])
            else:
                acc = psum.tile([P, S], F32, name="d_acc%d" % t, tag="bank%d" % t)
                parts = [(acc, 0, S)]
                for lo, hi in HALVES:
                    product(nc, acc[:, lo:hi], w_words[1], w_planes[1], t, two_codes[lo][:], two_scales[:, lo:hi])
            d_parts.append(parts)

        def gate_input(t):
            for acc, lo, hi in d_parts[t]:
                nc.scalar.copy(d_rows[t][:, lo:hi], acc[:])
                nc.scalar.copy(d_here[t][:, lo:hi], acc[:])
            for acc, lo, hi in d_parts[t]:
                nc.vector.tensor_tensor(diff[t][:, lo:hi], d_rows[t][:].indirect(entries(n2_l, lo, hi)), d_here[t][:, lo:hi], ALU.subtract)

        def blend_terms(t):
            y_acc = psum.tile([P, S], F32, name="y_acc%d" % t, tag="bank%d" % ((PACK + t) % 7))
            product(nc, y_acc[:], w_words[0], w_planes[0], t, idx_codes[:], idx_scales[:])
            nc.scalar.activation(pull[t][:], diff[t], ACT.Sigmoid)
            nc.scalar.activation(gy_rows[t][:, :S], y_acc[:], ACT.Copy, scale=gain[:, t : t + 1])
            nc.vector.tensor_tensor(far[:, t, :], gy_rows[t][:].indirect(n1_l[:]), pull[t][:], ALU.mult)
            nc.vector.scalar_tensor_tensor(near[:, t, :], pull[t][:], 1.0, gy_rows[t][:, :S], ALU.subtract, ALU.mult)

        gate_input(0)
        for t in range(PACK):
            if t + 1 < PACK:
                gate_input(t + 1)
            blend_terms(t)
        deal_plane(nc.vector, w_planes[2], raw_plane)

        h_acc = [psum.tile([P, S], F32, name="h_acc%d" % t, tag="bank%d" % (t + 1)) for t in range(PACK)]
        h_rows = d_rows[1:] + d_rows[:1]
        z_woven = [keep.tile([P, PACK * (hi - lo)], BF16, name="z_woven%d" % lo, align_bytes=64) for lo, hi in Z_PIECES]
        z_codes = [keep.tile([P, hi - lo], U32, name="z_codes%d" % lo, align_bytes=64) for lo, hi in Z_PIECES]
        z_scales = [keep.tile([P, hi - lo], U8, name="z_scales%d" % lo, align_bytes=64) for lo, hi in Z_PIECES]

        def blend(i):
            lo, hi = Z_PIECES[i]
            nc.vector.tensor_tensor(woven(z_woven[i]), by_pairs(far[:, :, lo:hi]), by_pairs(near[:, :, lo:hi]), ALU.subtract)

        def last_product(i):
            lo, hi = Z_PIECES[i]
            nc.vector.quantize_mx(out=z_codes[i][:].bitcast(FP8X4), scales=z_scales[i][:], in_=z_woven[i][:])
            for t in range(PACK):
                product(nc, h_acc[t][:, lo:hi], w_words[2], w_planes[2], t, z_codes[i][:], z_scales[i][:])
                if hi < S:
                    nc.scalar.copy(h_rows[t][:, lo:hi], h_acc[t][:, lo:hi])

        blend(0)
        for i in range(len(Z_PIECES)):
            if i + 1 < len(Z_PIECES):
                blend(i + 1)
            last_product(i)

        out_rows = out_0.rearrange("(p t) j -> p t j", t=PACK)
        out_words = out_1[0].rearrange("p j r -> p (j r)").bitcast(I32)
        o_scales = keep.tile([P, S], U8, align_bytes=64)
        o_codes = keep.tile([P, S], U32, align_bytes=64)
        mix = keep.tile([P, PACK, S], F32)
        rest = keep.tile([P, PACK, S], F32)
        term3 = keep.tile([P, PACK, S], F32)
        term5 = keep.tile([P, PACK, S], F32)
        result = keep.tile([P, PACK, S], F32)

        def weights(t, lo, hi):
            nc.scalar.activation(mix[:, t, lo:hi], h_rows[t][:].indirect(entries(n4_l, lo, hi)), ACT.Sigmoid)
            if lo or t:
                nc.scalar.activation(rest[:, t, lo:hi], mix[:, t, lo:hi], ACT.Copy, scale=-1.0, bias=1.0)

        def terms(t, lo, hi):
            if lo == 0 and t == 0:
                nc.vector.tensor_copy(term3[:, t, lo:hi], h_rows[t][:].indirect(entries(n3_l, lo, hi)))
                nc.vector.tensor_tensor(rest[:, t, lo:hi], h_rows[t][:].indirect(entries(n5_l, lo, hi)), term3[:, t, lo:hi], ALU.subtract)
                nc.vector.tensor_tensor(term5[:, t, lo:hi], rest[:, t, lo:hi], mix[:, t, lo:hi], ALU.mult)
            else:
                nc.vector.tensor_tensor(term5[:, t, lo:hi], h_rows[t][:].indirect(entries(n5_l, lo, hi)), mix[:, t, lo:hi], ALU.mult)
                nc.vector.tensor_tensor(term3[:, t, lo:hi], h_rows[t][:].indirect(entries(n3_l, lo, hi)), rest[:, t, lo:hi], ALU.mult)

        def add_terms(t0, t1, lo, hi):
            nc.vector.tensor_tensor(result[:, t0:t1, lo:hi], term3[:, t0:t1, lo:hi], term5[:, t0:t1, lo:hi], ALU.add)

        def add_terms_on_tensor(t):
            turned_sum = psum.tile([P, S], F32, name="turned_sum%d" % t, tag="bank%d" % (5 + t))
            for lo in range(0, S, P):
                nc.tensor.matmul(turned_sum[:, lo : lo + P], term5[:, t, lo : lo + P], ident[:], start=True, stop=False, is_transpose=True)
                nc.tensor.matmul(turned_sum[:, lo : lo + P], term3[:, t, lo : lo + P], ident[:], start=False, stop=True, is_transpose=True)
            turned = keep.tile([P, S], F32, name="turned%d" % t)
            nc.scalar.copy(turned[:], turned_sum[:])
            back = psum.tile([P, S], F32, name="back%d" % t, tag="bank%d" % (7 * t))
            for lo in range(0, S, P):
                nc.tensor.transpose(back[:, lo : lo + P], turned[:, lo : lo + P], ident[:])
            nc.scalar.copy(result[:, t, :], back[:])

        def store_rows(t0, t1, lo, hi):
            nc.sync.dma_start(out=out_rows[:, t0:t1, lo:hi], in_=result[:, t0:t1, lo:hi])

        def planes(lo, hi):
            o_woven = keep.tile([P, PACK * (hi - lo)], BF16, name="o_woven%d" % lo, align_bytes=64)
            if hi < S:
                nc.scalar.copy(woven(o_woven), by_pairs(result[:, :, lo:hi]))
            else:
                nc.vector.tensor_copy(woven(o_woven), by_pairs(result[:, :, lo:hi]))
            nc.vector.quantize_mx(out=o_codes[:, lo:hi].bitcast(FP8X4), scales=o_scales[:, lo:hi], in_=o_woven[:])

        last_lo = Z_PIECES[-1][0]
        for t in range(PACK):
            if t == 0:
                nc.vector.tensor_copy(h_rows[t][:, last_lo:S], h_acc[t][:, last_lo:S])
            else:
                nc.scalar.copy(h_rows[t][:, last_lo:S], h_acc[t][:, last_lo:S])
            for lo, hi in HALVES if t in (0, PACK - 1) else [(0, S)]:
                weights(t, lo, hi)
        for lo, hi in HALVES:
            terms(0, lo, hi)
        for t in range(1, PACK - 1):
            terms(t, 0, S)
        terms(PACK - 1, *OUT_PIECES[0])
        add_terms_on_tensor(0)
        add_terms_on_tensor(1)
        store_rows(0, 2, 0, S)
        add_terms(2, PACK - 1, 0, S)
        store_rows(2, PACK - 1, 0, S)
        add_terms(PACK - 1, PACK, *OUT_PIECES[0])
        for lo, hi in OUT_PIECES[1:]:
            terms(PACK - 1, lo, hi)
            add_terms(PACK - 1, PACK, lo, hi)
        store_rows(PACK - 1, PACK, 0, S)
        for lo, hi in OUT_PIECES:
            planes(lo, hi)
        nc.sync.dma_start(out=out_words, in_=o_codes[:].bitcast(I32))
        for q in range(4):
            queue = nc.scalar if q % 2 else nc.sync
            queue.dma_start(out=out_2[0, 4 * q : 4 * q + 4, :].bitcast(I32), in_=o_scales[32 * q : 32 * q + 4, :].bitcast(I32))
